import numpy as np
import ml_dtypes


def mxq(x, axis, fmt="e4m3"):
    dtype, down = {"e4m3": (ml_dtypes.float8_e4m3fn, 7), "e5m2": (ml_dtypes.float8_e5m2, 14)}[fmt]
    v = np.moveaxis(np.asarray(x, np.float32).astype(ml_dtypes.bfloat16).astype(np.float64), axis, -1)
    blocks = v.reshape(v.shape[:-1] + (-1, 32))
    amax = np.abs(blocks).max(-1, keepdims=True)
    byte = np.maximum(np.where(amax > 0, np.frexp(amax)[1] - 1 + 127, 0) - down, 1)
    scale = np.exp2(byte - 127.0)
    codes = (blocks / scale).astype(np.float32).astype(dtype).astype(np.float64)
    return np.moveaxis((codes * scale).reshape(v.shape), -1, axis)


WIDE = False


def mx_kscale(k):
    if not WIDE:
        return np.ones(k)
    levels = np.array([30, -30])
    if k % 512:
        return np.exp2(np.random.permutation(np.resize(levels, k // 32))).repeat(32)
    a = np.empty((k // 512, 16))
    for p in range(k // 512):
        a[p, :8] = np.random.permutation(np.resize(levels, 8))
        for g in range(8):
            far = levels[np.abs(levels - a[p, g]) >= 10]
            a[p, g + 8] = far[np.random.randint(len(far))]
    return np.exp2(a.ravel()).repeat(32)


def f64(x):
    return np.asarray(x).astype(np.float64)


K, L, M, N = 512, 1536, 1024, 1024


def setup_inputs():
    n = np.random.standard_normal
    s1 = mx_kscale(K)[:, None]
    s2 = mx_kscale(L)[:, None]
    m1, m2 = np.exp(0.5 * n((1, M))), np.exp(0.5 * n((1, N)))
    return {
        "x": (n((K, M)) / np.sqrt(K) * s1).astype(np.float32),
        "xt": (n((K, N)) / s1).astype(np.float32),
        "g": (m1 * n((L, M)) / np.sqrt(L) * s2).astype(np.float32),
        "gt": (m2 * n((L, N)) / s2).astype(np.float32),
    }


def reference(x, xt, g, gt):
    x_ = mxq(f64(x), 0, "e4m3")
    xt_ = mxq(f64(xt), 0, "e4m3")
    g_ = mxq(f64(g), 0, "e5m2")
    gt_ = mxq(f64(gt), 0, "e5m2")
    y = x_.T @ xt_
    u = g_.T @ gt_
    y = y * u
    return y

@@ -1,0 +1,176 @@
+from contextlib import ExitStack
+
+import concourse.mybir as mybir
+
+K, L, M, N = 512, 1536, 1024, 1024
+FLOPS = 2 * M * N * (K + L)
+
+F32 = mybir.dt.float32
+BF16 = mybir.dt.bfloat16
+U32 = mybir.dt.uint32
+U8 = mybir.dt.uint8
+E4M3 = mybir.dt.float8_e4m3fn_x4
+E5M2 = mybir.dt.float8_e5m2_x4
+MULT = mybir.AluOpType.mult
+
+P = 128
+PACK = 4
+K_PASS = P * PACK
+G_PASSES = L // K_PASS
+SUB = 256
+HALF = 512
+
+
+def tile_mix_ghost_none_kernel(tc, x, xt, g, gt, out):
+    nc = tc.nc
+    with ExitStack() as ctx:
+        keep = ctx.enter_context(tc.tile_pool(name="keep", bufs=1))
+        stage = ctx.enter_context(tc.tile_pool(name="stage", bufs=4))
+        psum = ctx.enter_context(tc.psum_pool(name="psum", bufs=8))
+        ctx.enter_context(tc.manual_schedule())
+
+        def load(name, src, c, c0, c1):
+            raw = keep.tile([P, PACK, c1 - c0], F32, name="raw_" + name)
+            rows = src[c * K_PASS : (c + 1) * K_PASS, c0:c1]
+            nc.sync.dma_start(out=raw[:], in_=rows.rearrange("(p j) w -> p j w", j=PACK))
+            return (raw, c0)
+
+        def operand(name, fmt):
+            codes = keep.tile([P, N], U32, name="codes_" + name, align_bytes=64)
+            scales = keep.tile([P, N], U8, name="scales_" + name, align_bytes=64)
+            return (codes, scales, fmt)
+
+        def interleave(piece, s, on_vector):
+            raw, c0 = piece
+            view = raw[:, :, s * SUB - c0 : (s + 1) * SUB - c0].rearrange("p j w -> p w j")
+            if on_vector:
+                grouped_v = stage.tile([P, SUB, PACK], BF16, align_bytes=64)
+                nc.vector.tensor_copy(out=grouped_v[:], in_=view)
+                return grouped_v
+            grouped_s = stage.tile([P, SUB, PACK], BF16, align_bytes=64)
+            nc.scalar.copy(out=grouped_s[:], in_=view)
+            return grouped_s
+
+        def quantize(op, s, grouped):
+            codes, scales, fmt = op
+            cols = slice(s * SUB, (s + 1) * SUB)
+            nc.vector.quantize_mx(
+                out=codes[:, cols].bitcast(fmt),
+                scales=scales[:, cols],
+                in_=grouped[:].rearrange("p w j -> p (w j)"),
+            )
+
+        def prepare(piece, op, order, on_scalar):
+            done = {}
+            for s in on_scalar:
+                done[s] = interleave(piece, s, False)
+            for what, s in order:
+                if what == "c":
+                    done[s] = interleave(piece, s, True)
+                else:
+                    quantize(op, s, done[s])
+
+        def multiply(acc, left, right, b, h, start, stop):
+            lc, ls, lf = left
+            rc, rs, rf = right
+            mc = slice(b * P, (b + 1) * P)
+            ncol = slice(h * HALF, (h + 1) * HALF)
+            nc.tensor.matmul_mx(
+                out=acc[:],
+                lhsT=lc[:, mc].bitcast(lf),
+                lhsT_scale=ls[:, mc],
+                rhs=rc[:, ncol].bitcast(rf),
+                rhs_scale=rs[:, ncol],
+                start=start,
+                stop=stop,
+            )
+
+        def new_acc():
+            acc = psum.tile([P, HALF], F32)
+            return acc
+
+        p_xt = load("xt", xt, 0, 0, N)
+        p_x = load("x", x, 0, 0, M)
+        p_gt = []
+        p_ga = []
+        for c in range(G_PASSES):
+            p_gt.append(load("gt%d" % c, gt, c, 0, N))
+            p_ga.append(load("g%da" % c, g, c, 0, HALF))
+        p_gb = [load("g%db" % c, g, c, HALF, M) for c in range(G_PASSES)]
+
+        o_xt = operand("xt", E4M3)
+        o_x = operand("x", E4M3)
+        o_gt = [operand("gt%d" % c, E5M2) for c in range(G_PASSES)]
+        o_g = [operand("g%d" % c, E5M2) for c in range(G_PASSES)]
+        result = [keep.tile([P, N], F32, name="result%d" % b) for b in range(M // P)]
+
+        two_two = [("c", 0), ("c", 1), ("q", 0), ("q", 2), ("q", 1), ("q", 3)]
+        three_one = [("c", 0), ("c", 1), ("q", 0), ("c", 2), ("q", 1), ("q", 3), ("q", 2)]
+
+        tiles = [(b, h) for b in range(M // P) for h in range(2)]
+        first, second = tiles[:8], tiles[8:]
+
+        def a_tiles(some):
+            for b, h in some:
+                acc = new_acc()
+                multiply(acc, o_x, o_xt, b, h, True, True)
+                nc.scalar.copy(out=result[b][:, h * HALF : (h + 1) * HALF], in_=acc[:])
+
+        def u_pass(accs, some, c):
+            for b, h in some:
+                if c == 0:
+                    accs[(b, h)] = new_acc()
+                multiply(accs[(b, h)], o_g[c], o_gt[c], b, h, c == 0, c == G_PASSES - 1)
+
+        def finish(accs, some):
+            for b, h in some:
+                cols = slice(h * HALF, (h + 1) * HALF)
+                nc.vector.tensor_tensor(
+                    out=result[b][:, cols], in0=accs[(b, h)][:], in1=result[b][:, cols], op=MULT
+                )
+
+        def finish_g(accs, some):
+            for b, h in some:
+                cols = slice(h * HALF, (h + 1) * HALF)
+                moved = stage.tile([P, HALF], F32)
+                nc.scalar.copy(out=moved[:], in_=accs[(b, h)][:])
+                nc.gpsimd.tensor_tensor(out=result[b][:, cols], in0=moved[:], in1=result[b][:, cols], op=MULT)
+
+        def store(b):
+            nc.sync.dma_start(out=out[b * P : (b + 1) * P, :], in_=result[b][:])
+
+        low = [("c", 0), ("q", 1), ("q", 0)]
+        acc_a = {}
+        acc_b = {}
+        prepare(p_xt, o_xt, two_two, [2, 3])
+        prepare(p_x, o_x, two_two, [2, 3])
+        a_tiles(tiles[0:4])
+        prepare(p_gt[0], o_gt[0], three_one, [3])
+        a_tiles(tiles[4:8])
+        prepare(p_ga[0], o_g[0], low, [1])
+        a_tiles(tiles[8:16])
+        u_pass(acc_a, first, 0)
+        prepare(p_gt[1], o_gt[1], three_one, [3])
+        prepare(p_ga[1], o_g[1], low, [1])
+        u_pass(acc_a, first, 1)
+        prepare(p_gt[2], o_gt[2], three_one, [3])
+        prepare(p_ga[2], o_g[2], low, [1])
+        u_pass(acc_a, first, 2)
+        finish(acc_a, first[0:3])
+        gb0 = [interleave(p_gb[0], s, False) for s in (2, 3)]
+        quantize(o_g[0], 2, gb0[0])
+        finish(acc_a, first[3:5])
+        quantize(o_g[0], 3, gb0[1])
+        finish(acc_a, first[5:8])
+        u_pass(acc_b, second, 0)
+        prepare(p_gb[1], o_g[1], [("c", 2), ("q", 3), ("q", 2)], [3])
+        u_pass(acc_b, second, 1)
+        prepare(p_gb[2], o_g[2], [("c", 2), ("q", 3), ("q", 2)], [3])
+        u_pass(acc_b, second, 2)
+        for k in range(8):
+            if k in (2, 5):
+                finish_g(acc_b, second[k : k + 1])
+            else:
+                finish(acc_b, second[k : k + 1])
+        for b in range(M // P):
+            store(b)

@@ -25,7 +25,7 @@ def tile_mix_ghost_none_kernel(tc, x, xt, g, gt, out):
     nc = tc.nc
     with ExitStack() as ctx:
         keep = ctx.enter_context(tc.tile_pool(name="keep", bufs=1))
-        stage = ctx.enter_context(tc.tile_pool(name="stage", bufs=4))
+        stage = ctx.enter_context(tc.tile_pool(name="stage", bufs=5))
         psum = ctx.enter_context(tc.psum_pool(name="psum", bufs=8))
         ctx.enter_context(tc.manual_schedule())
 
@@ -91,12 +91,10 @@ def tile_mix_ghost_none_kernel(tc, x, xt, g, gt, out):
 
         p_xt = load("xt", xt, 0, 0, N)
         p_x = load("x", x, 0, 0, M)
-        p_gt = []
-        p_ga = []
-        for c in range(G_PASSES):
-            p_gt.append(load("gt%d" % c, gt, c, 0, N))
-            p_ga.append(load("g%da" % c, g, c, 0, HALF))
-        p_gb = [load("g%db" % c, g, c, HALF, M) for c in range(G_PASSES)]
+        p_gt = [load("gt%d" % c, gt, c, 0, N) for c in range(G_PASSES)]
+        p_ga = [load("g%da" % c, g, c, 0, HALF) for c in range(G_PASSES)]
+        p_gb = [load("g%db" % c, g, c, HALF, HALF + SUB) for c in range(G_PASSES)]
+        p_gc = [load("g%dc" % c, g, c, HALF + SUB, M) for c in range(G_PASSES)]
 
         o_xt = operand("xt", E4M3)
         o_x = operand("x", E4M3)
@@ -122,6 +120,12 @@ def tile_mix_ghost_none_kernel(tc, x, xt, g, gt, out):
                     accs[(b, h)] = new_acc()
                 multiply(accs[(b, h)], o_g[c], o_gt[c], b, h, c == 0, c == G_PASSES - 1)
 
+        def u_tile(accs, some):
+            for b, h in some:
+                accs[(b, h)] = new_acc()
+                for c in range(G_PASSES):
+                    multiply(accs[(b, h)], o_g[c], o_gt[c], b, h, c == 0, c == G_PASSES - 1)
+
         def finish(accs, some):
             for b, h in some:
                 cols = slice(h * HALF, (h + 1) * HALF)
@@ -139,38 +143,50 @@ def tile_mix_ghost_none_kernel(tc, x, xt, g, gt, out):
         def store(b):
             nc.sync.dma_start(out=out[b * P : (b + 1) * P, :], in_=result[b][:])
 
-        low = [("c", 0), ("q", 1), ("q", 0)]
-        acc_a = {}
-        acc_b = {}
-        prepare(p_xt, o_xt, two_two, [2, 3])
-        prepare(p_x, o_x, two_two, [2, 3])
-        a_tiles(tiles[0:4])
-        prepare(p_gt[0], o_gt[0], three_one, [3])
-        a_tiles(tiles[4:8])
-        prepare(p_ga[0], o_g[0], low, [1])
-        a_tiles(tiles[8:16])
-        u_pass(acc_a, first, 0)
-        prepare(p_gt[1], o_gt[1], three_one, [3])
-        prepare(p_ga[1], o_g[1], low, [1])
-        u_pass(acc_a, first, 1)
-        prepare(p_gt[2], o_gt[2], three_one, [3])
-        prepare(p_ga[2], o_g[2], low, [1])
-        u_pass(acc_a, first, 2)
-        finish(acc_a, first[0:3])
-        gb0 = [interleave(p_gb[0], s, False) for s in (2, 3)]
-        quantize(o_g[0], 2, gb0[0])
-        finish(acc_a, first[3:5])
-        quantize(o_g[0], 3, gb0[1])
-        finish(acc_a, first[5:8])
-        u_pass(acc_b, second, 0)
-        prepare(p_gb[1], o_g[1], [("c", 2), ("q", 3), ("q", 2)], [3])
-        u_pass(acc_b, second, 1)
-        prepare(p_gb[2], o_g[2], [("c", 2), ("q", 3), ("q", 2)], [3])
-        u_pass(acc_b, second, 2)
-        for k in range(8):
-            if k in (2, 5):
-                finish_g(acc_b, second[k : k + 1])
-            else:
-                finish(acc_b, second[k : k + 1])
-        for b in range(M // P):
+        prepare(p_xt, o_xt, two_two, [3, 2])
+        prepare(p_x, o_x, two_two, [3, 2])
+        a_tiles(tiles)
+        all_v = [("c", 0), ("c", 1), ("q", 0), ("q", 1), ("c", 2), ("c", 3), ("q", 2), ("q", 3)]
+        prepare(p_gt[0], o_gt[0], all_v, [])
+        prepare(p_gt[1], o_gt[1], all_v, [])
+        gt3 = interleave(p_gt[2], 3, False)
+        gt2 = interleave(p_gt[2], 2, False)
+        gt0 = interleave(p_gt[2], 0, True)
+        gt1 = interleave(p_gt[2], 1, True)
+        quantize(o_gt[2], 0, gt0)
+        quantize(o_gt[2], 1, gt1)
+        quantize(o_gt[2], 3, gt3)
+        a0 = interleave(p_ga[0], 0, True)
+        a1 = interleave(p_ga[0], 1, False)
+        quantize(o_gt[2], 2, gt2)
+        quantize(o_g[0], 0, a0)
+        accs = {}
+        u_pass(accs, first[0:4], 0)
+        for c in (1, 2):
+            nxt0 = interleave(p_ga[c], 0, True)
+            nxt1 = interleave(p_ga[c], 1, False)
+            quantize(o_g[c - 1], 1, a1)
+            u_pass(accs, first[4:8], c - 1)
+            quantize(o_g[c], 0, nxt0)
+            u_pass(accs, first[0:4], c)
+            a1 = nxt1
+        b0 = interleave(p_gb[0], 2, True)
+        quantize(o_g[2], 1, a1)
+        u_pass(accs, first[4:8], 2)
+        quantize(o_g[0], 2, b0)
+        late = [(p_gb[1], 1, 2), (p_gb[2], 2, 2), (p_gc[0], 0, 3), (p_gc[1], 1, 3), (p_gc[2], 2, 3)]
+        moved_late = [interleave(piece, s, False) for piece, c, s in late]
+        for n in range(8):
+            finish(accs, tiles[2 * n : 2 * n + 2])
+            if n < len(late):
+                quantize(o_g[late[n][1]], late[n][2], moved_late[n])
+            if n == 1:
+                u_tile(accs, tiles[8:12])
+            if n == 4:
+                u_tile(accs, tiles[12:16])
+        for b in range(M // P - 2):
             store(b)
+        for b in range(M // P - 2, M // P):
+            for h in range(2):
+                cols = slice(h * HALF, (h + 1) * HALF)
+                nc.sync.dma_start(out=out[b * P : (b + 1) * P, cols], in_=result[b][:, cols])

from contextlib import ExitStack

import concourse.mybir as mybir

K, L, M, N = 512, 1536, 1024, 1024
FLOPS = 2 * M * N * (K + L)

F32 = mybir.dt.float32
BF16 = mybir.dt.bfloat16
U32 = mybir.dt.uint32
U8 = mybir.dt.uint8
E4M3 = mybir.dt.float8_e4m3fn_x4
E5M2 = mybir.dt.float8_e5m2_x4
MULT = mybir.AluOpType.mult

P = 128
PACK = 4
K_PASS = P * PACK
G_PASSES = L // K_PASS
SUB = 256
HALF = 512


def tile_mix_ghost_none_kernel(tc, x, xt, g, gt, out):
    nc = tc.nc
    with ExitStack() as ctx:
        keep = ctx.enter_context(tc.tile_pool(name="keep", bufs=1))
        stage = ctx.enter_context(tc.tile_pool(name="stage", bufs=5))
        psum = ctx.enter_context(tc.psum_pool(name="psum", bufs=8))
        ctx.enter_context(tc.manual_schedule())

        def load(name, src, c, c0, c1):
            raw = keep.tile([P, PACK, c1 - c0], F32, name="raw_" + name)
            rows = src[c * K_PASS : (c + 1) * K_PASS, c0:c1]
            nc.sync.dma_start(out=raw[:], in_=rows.rearrange("(p j) w -> p j w", j=PACK))
            return (raw, c0)

        def operand(name, fmt):
            codes = keep.tile([P, N], U32, name="codes_" + name, align_bytes=64)
            scales = keep.tile([P, N], U8, name="scales_" + name, align_bytes=64)
            return (codes, scales, fmt)

        def interleave(piece, s, on_vector):
            raw, c0 = piece
            view = raw[:, :, s * SUB - c0 : (s + 1) * SUB - c0].rearrange("p j w -> p w j")
            if on_vector:
                grouped_v = stage.tile([P, SUB, PACK], BF16, align_bytes=64)
                nc.vector.tensor_copy(out=grouped_v[:], in_=view)
                return grouped_v
            grouped_s = stage.tile([P, SUB, PACK], BF16, align_bytes=64)
            nc.scalar.copy(out=grouped_s[:], in_=view)
            return grouped_s

        def quantize(op, s, grouped):
            codes, scales, fmt = op
            cols = slice(s * SUB, (s + 1) * SUB)
            nc.vector.quantize_mx(
                out=codes[:, cols].bitcast(fmt),
                scales=scales[:, cols],
                in_=grouped[:].rearrange("p w j -> p (w j)"),
            )

        def prepare(piece, op, order, on_scalar):
            done = {}
            for s in on_scalar:
                done[s] = interleave(piece, s, False)
            for what, s in order:
                if what == "c":
                    done[s] = interleave(piece, s, True)
                else:
                    quantize(op, s, done[s])

        def multiply(acc, left, right, b, h, start, stop):
            lc, ls, lf = left
            rc, rs, rf = right
            mc = slice(b * P, (b + 1) * P)
            ncol = slice(h * HALF, (h + 1) * HALF)
            nc.tensor.matmul_mx(
                out=acc[:],
                lhsT=lc[:, mc].bitcast(lf),
                lhsT_scale=ls[:, mc],
                rhs=rc[:, ncol].bitcast(rf),
                rhs_scale=rs[:, ncol],
                start=start,
                stop=stop,
            )

        def new_acc():
            acc = psum.tile([P, HALF], F32)
            return acc

        p_xt = load("xt", xt, 0, 0, N)
        p_x = load("x", x, 0, 0, M)
        p_gt = [load("gt%d" % c, gt, c, 0, N) for c in range(G_PASSES)]
        p_ga = [load("g%da" % c, g, c, 0, HALF) for c in range(G_PASSES)]
        p_gb = [load("g%db" % c, g, c, HALF, HALF + SUB) for c in range(G_PASSES)]
        p_gc = [load("g%dc" % c, g, c, HALF + SUB, M) for c in range(G_PASSES)]

        o_xt = operand("xt", E4M3)
        o_x = operand("x", E4M3)
        o_gt = [operand("gt%d" % c, E5M2) for c in range(G_PASSES)]
        o_g = [operand("g%d" % c, E5M2) for c in range(G_PASSES)]
        result = [keep.tile([P, N], F32, name="result%d" % b) for b in range(M // P)]

        two_two = [("c", 0), ("c", 1), ("q", 0), ("q", 2), ("q", 1), ("q", 3)]
        three_one = [("c", 0), ("c", 1), ("q", 0), ("c", 2), ("q", 1), ("q", 3), ("q", 2)]

        tiles = [(b, h) for b in range(M // P) for h in range(2)]
        first, second = tiles[:8], tiles[8:]

        def a_tiles(some):
            for b, h in some:
                acc = new_acc()
                multiply(acc, o_x, o_xt, b, h, True, True)
                nc.scalar.copy(out=result[b][:, h * HALF : (h + 1) * HALF], in_=acc[:])

        def u_pass(accs, some, c):
            for b, h in some:
                if c == 0:
                    accs[(b, h)] = new_acc()
                multiply(accs[(b, h)], o_g[c], o_gt[c], b, h, c == 0, c == G_PASSES - 1)

        def u_tile(accs, some):
            for b, h in some:
                accs[(b, h)] = new_acc()
                for c in range(G_PASSES):
                    multiply(accs[(b, h)], o_g[c], o_gt[c], b, h, c == 0, c == G_PASSES - 1)

        def finish(accs, some):
            for b, h in some:
                cols = slice(h * HALF, (h + 1) * HALF)
                nc.vector.tensor_tensor(
                    out=result[b][:, cols], in0=accs[(b, h)][:], in1=result[b][:, cols], op=MULT
                )

        def finish_g(accs, some):
            for b, h in some:
                cols = slice(h * HALF, (h + 1) * HALF)
                moved = stage.tile([P, HALF], F32)
                nc.scalar.copy(out=moved[:], in_=accs[(b, h)][:])
                nc.gpsimd.tensor_tensor(out=result[b][:, cols], in0=moved[:], in1=result[b][:, cols], op=MULT)

        def store(b):
            nc.sync.dma_start(out=out[b * P : (b + 1) * P, :], in_=result[b][:])

        prepare(p_xt, o_xt, two_two, [3, 2])
        prepare(p_x, o_x, two_two, [3, 2])
        a_tiles(tiles)
        all_v = [("c", 0), ("c", 1), ("q", 0), ("q", 1), ("c", 2), ("c", 3), ("q", 2), ("q", 3)]
        prepare(p_gt[0], o_gt[0], all_v, [])
        prepare(p_gt[1], o_gt[1], all_v, [])
        gt3 = interleave(p_gt[2], 3, False)
        gt2 = interleave(p_gt[2], 2, False)
        gt0 = interleave(p_gt[2], 0, True)
        gt1 = interleave(p_gt[2], 1, True)
        quantize(o_gt[2], 0, gt0)
        quantize(o_gt[2], 1, gt1)
        quantize(o_gt[2], 3, gt3)
        a0 = interleave(p_ga[0], 0, True)
        a1 = interleave(p_ga[0], 1, False)
        quantize(o_gt[2], 2, gt2)
        quantize(o_g[0], 0, a0)
        accs = {}
        u_pass(accs, first[0:4], 0)
        for c in (1, 2):
            nxt0 = interleave(p_ga[c], 0, True)
            nxt1 = interleave(p_ga[c], 1, False)
            quantize(o_g[c - 1], 1, a1)
            u_pass(accs, first[4:8], c - 1)
            quantize(o_g[c], 0, nxt0)
            u_pass(accs, first[0:4], c)
            a1 = nxt1
        b0 = interleave(p_gb[0], 2, True)
        quantize(o_g[2], 1, a1)
        u_pass(accs, first[4:8], 2)
        quantize(o_g[0], 2, b0)
        late = [(p_gb[1], 1, 2), (p_gb[2], 2, 2), (p_gc[0], 0, 3), (p_gc[1], 1, 3), (p_gc[2], 2, 3)]
        moved_late = [interleave(piece, s, False) for piece, c, s in late]
        for n in range(8):
            finish(accs, tiles[2 * n : 2 * n + 2])
            if n < len(late):
                quantize(o_g[late[n][1]], late[n][2], moved_late[n])
            if n == 1:
                u_tile(accs, tiles[8:12])
            if n == 4:
                u_tile(accs, tiles[12:16])
        for b in range(M // P - 2):
            store(b)
        for b in range(M // P - 2, M // P):
            for h in range(2):
                cols = slice(h * HALF, (h + 1) * HALF)
                nc.sync.dma_start(out=out[b * P : (b + 1) * P, cols], in_=result[b][:, cols])
